import numpy as np
import ml_dtypes


def mxq(x, axis, fmt="e4m3"):
    dtype, down = {"e4m3": (ml_dtypes.float8_e4m3fn, 7), "e5m2": (ml_dtypes.float8_e5m2, 14)}[fmt]
    v = np.moveaxis(np.asarray(x, np.float32).astype(ml_dtypes.bfloat16).astype(np.float64), axis, -1)
    blocks = v.reshape(v.shape[:-1] + (-1, 32))
    amax = np.abs(blocks).max(-1, keepdims=True)
    byte = np.maximum(np.where(amax > 0, np.frexp(amax)[1] - 1 + 127, 0) - down, 1)
    scale = np.exp2(byte - 127.0)
    codes = (blocks / scale).astype(np.float32).astype(dtype).astype(np.float64)
    return np.moveaxis((codes * scale).reshape(v.shape), -1, axis)


WIDE = False


def mx_kscale(k):
    if not WIDE:
        return np.ones(k)
    levels = np.array([10, -10, 5, -5, 0])
    if k % 512:
        return np.exp2(np.random.permutation(np.resize(levels, k // 32))).repeat(32)
    a = np.empty((k // 512, 16))
    for p in range(k // 512):
        a[p, :8] = np.random.permutation(np.resize(levels, 8))
        for g in range(8):
            far = levels[np.abs(levels - a[p, g]) >= 10]
            a[p, g + 8] = far[np.random.randint(len(far))]
    return np.exp2(a.ravel()).repeat(32)


def f64(x):
    return np.asarray(x).astype(np.float64)


def striped(idx):
    return np.tile(idx.reshape(-1, 16).T, (8, 1)).astype(np.uint16)


def unstriped(offs):
    return offs[:16].T.reshape(-1).astype(np.int64)


E2M1 = np.array([0.0, 0.5, 1.0, 1.5, 2.0, 3.0, 4.0, 6.0, -0.0, -0.5, -1.0, -1.5, -2.0, -3.0, -4.0, -6.0])


def pack_weight(w, fmt):
    k, n = w.shape
    w = f64(np.asarray(w, np.float32).astype(ml_dtypes.bfloat16)).reshape(k // 32, 32, n)
    amax = np.abs(w).max(1)
    if fmt == "e4m3":
        byte = np.frexp(amax)[1] - 1 + 127 - 7
    else:
        mant, ex = np.frexp(amax / 6.0)
        byte = np.where(mant > 0.5, ex, ex - 1) + 127
    byte = np.clip(np.where(amax > 0, byte, 1), 1, 254)
    scaled = (w * np.exp2(127.0 - byte)[:, None, :]).reshape(k, n).astype(np.float32)
    by_word = np.ascontiguousarray(scaled.reshape(k // 512, 128, 4, n).transpose(0, 1, 3, 2))
    if fmt == "e4m3":
        words = by_word.astype(ml_dtypes.float8_e4m3fn).view(np.uint8)
    else:
        c = by_word.astype(ml_dtypes.float4_e2m1fn).view(np.uint8) & 0xF
        words = (c[..., 0::2] | (c[..., 1::2] << 4)).reshape(k // 512, 128, 2 * n)
    return np.ascontiguousarray(words), np.ascontiguousarray(byte.astype(np.uint8).reshape(k // 512, 16, n))


def unpack_weight(words, scales, fmt):
    g, _, n = scales.shape
    words = np.ascontiguousarray(words).reshape(g, 128, n, -1)
    if fmt == "e4m3":
        vals = words.view(ml_dtypes.float8_e4m3fn).astype(np.float64)
    else:
        nib = np.empty((g, 128, n, 4), np.uint8)
        nib[..., 0::2] = words & 0xF
        nib[..., 1::2] = words >> 4
        vals = E2M1[nib]
    vals = vals * np.repeat(np.exp2(scales.astype(np.float64) - 127.0), 8, axis=1)[..., None]
    return vals.transpose(0, 1, 3, 2).reshape(g * 512, n)


def gelu(v):
    return 0.5 * v * (1.0 + np.tanh(np.sqrt(2.0 / np.pi) * (v + 0.044715 * v**3)))


def bf(x):
    return np.asarray(x, np.float32).astype(ml_dtypes.bfloat16)


def planes(Y):
    n, m = Y.shape
    b = f64(bf(Y)).reshape(n // 32, 32, m)
    amax = np.abs(b).max(1)
    byte = np.clip(np.where(amax > 0, np.frexp(amax)[1] - 1 + 127 - 7, 1), 1, 254)
    codes = (b * np.exp2(127.0 - byte)[:, None, :]).reshape(n, m).astype(np.float32).astype(ml_dtypes.float8_e4m3fn).view(np.uint8)
    words = codes.reshape(n // 512, 128, 4, m).transpose(0, 1, 3, 2)
    return np.ascontiguousarray(words), np.ascontiguousarray(byte.astype(np.uint8).reshape(n // 512, 16, m))


K, H, N, T, S, P = 512, 1536, 1024, 4096, 1024, 512

def setup_inputs():
    n = np.random.standard_normal
    s = mx_kscale(K)[:, None]
    u = mx_kscale(H)[:, None]
    tab_words, tab_scales = pack_weight(n((K, T)) * s, "e4m3")
    w1 = n((K, H)) / np.sqrt(K) / s * u.T
    low = (0.5 * n(H) - 0.4) * u[:, 0]
    wa_words, wa_scales = pack_weight(1.2 * n((H, N)) / np.sqrt(H) / u, "e2m1")
    return {
        "tab_words": tab_words, "tab_scales": tab_scales,
        "offs": striped(np.random.permutation(T)[:S]),
        "pos1": striped(np.random.permutation(S)[:P]),
        "pos2": striped(np.random.permutation(S)[:P]),
        "w1": w1.astype(np.float32),
        "low": low.astype(np.float32),
        "wa_words": wa_words, "wa_scales": wa_scales,
        "limit": n(N).astype(np.float32),
        "clear": (0.5 * n((N, P))).astype(np.float32),
        "gain": np.exp(0.8 * n(N)).astype(np.float32),
    }

def reference(tab_words, tab_scales, offs, pos1, pos2, w1, low, wa_words, wa_scales, limit, clear, gain):
    v = unpack_weight(tab_words, tab_scales, "e4m3")[:, unstriped(offs)]
    h = mxq(f64(w1), 0, "e4m3").T @ v
    h = np.maximum(h, f64(low)[:, None])
    wa = unpack_weight(wa_words, wa_scales, "e2m1")
    e = wa.T @ mxq(h, 0, "e4m3")
    a = 1.0 / (1.0 + np.exp(-(e[:, unstriped(pos1)] + f64(limit)[:, None])))
    c = np.maximum(e[:, unstriped(pos2)], f64(clear))
    y = f64(gain)[:, None] * (c - a)
    words, scales = planes(y)
    return y, words, scales

@@ -1,0 +1,272 @@
+from contextlib import ExitStack
+
+import concourse.mybir as mybir
+
+K, H, N, T, S, M = 512, 1536, 1024, 4096, 1024, 512
+FLOPS = 2 * K * H * S + 2 * H * N * S
+
+F32 = mybir.dt.float32
+BF16 = mybir.dt.bfloat16
+I32 = mybir.dt.int32
+U32 = mybir.dt.uint32
+U16 = mybir.dt.uint16
+U8 = mybir.dt.uint8
+FP8X4 = mybir.dt.float8_e4m3fn_x4
+FP4X4 = mybir.dt.float4_e2m1fn_x4
+ALU = mybir.AluOpType
+ACT = mybir.ActivationFunctionType
+
+P = 128
+PACK = 4
+PASS = P * PACK
+H_PASSES = H // PASS
+N_GROUPS = N // PASS
+SUB = 128
+CHUNK = 256
+EARLY = 2
+
+
+def tile_list_fog_hours_kernel(
+    tc, tab_words, tab_scales, offs, pos1, pos2, w1, low, wa_words, wa_scales, limit, clear, gain, out_0, out_1, out_2
+):
+    nc = tc.nc
+    with ExitStack() as ctx:
+        keep = ctx.enter_context(tc.tile_pool(name="keep", bufs=1))
+        ring = ctx.enter_context(tc.tile_pool(name="ring", bufs=3))
+        ps1 = ctx.enter_context(tc.psum_pool(name="ps1", bufs=4))
+        ps2 = ctx.enter_context(tc.psum_pool(name="ps2", bufs=4))
+
+        offs_sb = keep.tile([P, S // 16], U16, name="offs_sb")
+        pos1_sb = keep.tile([P, M // 16], U16, name="pos1_sb")
+        pos2_sb = keep.tile([P, M // 16], U16, name="pos2_sb")
+        tabw = keep.tile([P, T], I32, name="tabw", align_bytes=64)
+        tabs = keep.tile([P, T], U8, name="tabs", align_bytes=64)
+        was_raw = keep.tile([P, H_PASSES * N], U8, name="was_raw", align_bytes=64)
+        nc.vector.memset(tabs[:].bitcast(I32), 0)
+        nc.gpsimd.memset(was_raw[:].bitcast(I32), 0)
+
+        nc.sync.dma_start(tabw[:], tab_words[0].rearrange("p n t -> p (n t)").bitcast(I32))
+        nc.sync.dma_start(offs_sb[:], offs)
+        for q in range(4):
+            nc.sync.dma_start(tabs[32 * q : 32 * q + 4, :].bitcast(I32), tab_scales[0, 4 * q : 4 * q + 4, :].bitcast(I32))
+
+        w1_view = w1.rearrange("(p j) c -> p j c", j=PACK)
+        w1_parts = []
+        for b in range(H_PASSES):
+            cuts = (0, 256, 384, PASS) if b == 0 else (0, PASS)
+            parts = []
+            for c0, c1 in zip(cuts[:-1], cuts[1:]):
+                raw = keep.tile([P, PACK, c1 - c0], F32, name=f"w1raw{b}_{c0}")
+                nc.sync.dma_start(raw[:], w1_view[:, :, b * PASS + c0 : b * PASS + c1])
+                parts.append((c0, c1, raw))
+            w1_parts.append(parts)
+            if b == 1:
+                for q in range(4):
+                    nc.sync.dma_start(
+                        was_raw[32 * q : 32 * q + 4, :].bitcast(I32).rearrange("r (a c) -> r a c", a=H_PASSES),
+                        wa_scales[:, 4 * q : 4 * q + 4, :].bitcast(I32).rearrange("a r c -> r a c"),
+                    )
+
+        low_sb = keep.tile([P, H_PASSES, PACK], F32, name="low_sb")
+        limit_sb = keep.tile([P, N_GROUPS * PACK], F32, name="limit_sb")
+        gain_sb = keep.tile([P, N_GROUPS * PACK], F32, name="gain_sb")
+        nc.gpsimd.dma_start(low_sb[:], low.rearrange("(b p t) -> p b t", p=P, t=PACK))
+        nc.gpsimd.dma_start(limit_sb[:].rearrange("p (g t) -> p g t", t=PACK), limit.rearrange("(g p t) -> p g t", p=P, t=PACK))
+        nc.gpsimd.dma_start(gain_sb[:].rearrange("p (g t) -> p g t", t=PACK), gain.rearrange("(g p t) -> p g t", p=P, t=PACK))
+
+        waw_raw = []
+        for g in range(N_GROUPS):
+            raw = keep.tile([P, H_PASSES * PASS // 2], I32, name=f"waw_raw{g}")
+            nc.sync.dma_start(
+                raw[:].rearrange("p (a c) -> p a c", a=H_PASSES),
+                wa_words[:, :, 2 * g * PASS : 2 * (g + 1) * PASS].bitcast(I32).rearrange("a p c -> p a c"),
+            )
+            waw_raw.append(raw)
+        nc.sync.dma_start(pos1_sb[:], pos1)
+        nc.sync.dma_start(pos2_sb[:], pos2)
+        clear_view = clear.rearrange("(g p t) m -> g p t m", p=P, t=PACK)
+        clear_sb = []
+        for g in range(N_GROUPS):
+            ct = keep.tile([P, PACK, M], F32, name=f"clear{g}")
+            nc.sync.dma_start(ct[:], clear_view[g])
+            clear_sb.append(ct)
+
+        vw, vs = [], []
+        for half in range(2):
+            cols = offs_sb[:, half * 32 : (half + 1) * 32]
+            wt = keep.tile([P, S // 2], U32, name=f"vw{half}", align_bytes=64)
+            st = keep.tile([P, S // 2], U8, name=f"vs{half}", align_bytes=64)
+            nc.vector.tensor_copy(wt[:], tabw[:].bitcast(U32).indirect(cols))
+            nc.vector.tensor_copy(st[:], tabs[:].indirect(cols))
+            vw.append(wt)
+            vs.append(st)
+
+        w1c, w1s, w1bf = [], [], []
+        for b in range(H_PASSES):
+            bf = keep.tile([P, PACK * PASS], BF16, name=f"w1bf{b}", align_bytes=64)
+            dealt = bf[:].rearrange("p (t m j) -> p m j t", t=PACK, j=PACK)
+            for c0, c1, raw in w1_parts[b]:
+                nc.scalar.copy(dealt[:, c0 // PACK : c1 // PACK, :, :], raw[:].rearrange("p j (m t) -> p m j t", t=PACK))
+            w1bf.append(bf)
+            w1c.append(keep.tile([P, PASS], U32, name=f"w1c{b}", align_bytes=64))
+            w1s.append(keep.tile([P, PASS], U8, name=f"w1s{b}", align_bytes=64))
+
+        def quantize_w1(b):
+            nc.vector.quantize_mx(out=w1c[b][:].bitcast(FP8X4), scales=w1s[b][:], in_=w1bf[b][:])
+
+        waw = [[None] * N_GROUPS for a in range(H_PASSES)]
+        was = [[None] * N_GROUPS for a in range(H_PASSES)]
+        for g in range(N_GROUPS):
+            for a in range(H_PASSES):
+                st = keep.tile([P, PASS], U8, name=f"was{a}_{g}", align_bytes=64)
+                src = was_raw[:, a * N + g * PASS : a * N + (g + 1) * PASS]
+                nc.gpsimd.tensor_copy(st[:].rearrange("p (t q) -> p t q", t=PACK), src.rearrange("p (q t) -> p t q", t=PACK))
+                was[a][g] = st
+        for g in range(N_GROUPS):
+            wt = keep.tile([P, H_PASSES * 2 * PASS], U8, name=f"waw{g}", align_bytes=64)
+            nc.scalar.copy(
+                wt[:].bitcast(U16).rearrange("p (a t q) -> p a t q", a=H_PASSES, t=PACK),
+                waw_raw[g][:].bitcast(U16).rearrange("p (a q t) -> p a t q", a=H_PASSES, t=PACK),
+            )
+            for a in range(H_PASSES):
+                waw[a][g] = wt[:, 2 * a * PASS : 2 * (a + 1) * PASS]
+
+        e_sb = [keep.tile([P, S], F32, name=f"e{i}") for i in range(N_GROUPS * PACK)]
+        hc = [[keep.tile([P, S // 2], U32, name=f"hc{half}_{b}", align_bytes=64) for b in range(H_PASSES)] for half in range(2)]
+        hs = [[keep.tile([P, S // 2], U8, name=f"hs{half}_{b}", align_bytes=64) for b in range(H_PASSES)] for half in range(2)]
+        hbf = {}
+
+        def stage1(ci, b):
+            bf = ring.tile([P, PACK * CHUNK], BF16, name="hbf", align_bytes=64)
+            hbf[(ci, b)] = bf
+            for u in range(CHUNK // SUB):
+                col = ci * CHUNK + u * SUB
+                half, c0 = divmod(col, S // 2)
+                bank = ps1.tile([P, PACK, SUB], F32, name="bank1")
+                for t in range(PACK):
+                    nc.tensor.matmul_mx(
+                        out=bank[:, t, :],
+                        lhsT=w1c[b][:, t * P : (t + 1) * P].bitcast(FP8X4),
+                        lhsT_scale=w1s[b][:, t * P : (t + 1) * P],
+                        rhs=vw[half][:, c0 : c0 + SUB].bitcast(FP8X4),
+                        rhs_scale=vs[half][:, c0 : c0 + SUB],
+                        start=True,
+                        stop=True,
+                    )
+                nc.vector.tensor_tensor(
+                    bf[:, u * PACK * SUB : (u + 1) * PACK * SUB].rearrange("p (j t) -> p j t", t=PACK),
+                    bank[:].rearrange("p t j -> p j t"),
+                    low_sb[:, b : b + 1, :].to_broadcast([P, SUB, PACK]),
+                    ALU.max,
+                )
+
+        def quantize_h(ci, b):
+            half, c0 = divmod(ci * CHUNK, S // 2)
+            nc.vector.quantize_mx(
+                out=hc[half][b][:, c0 : c0 + CHUNK].bitcast(FP8X4), scales=hs[half][b][:, c0 : c0 + CHUNK], in_=hbf[(ci, b)][:]
+            )
+
+        def stage2(i, s0, width, on_vector):
+            half, c0 = divmod(s0, S // 2)
+            g, t = divmod(i, PACK)
+            bank = ps2.tile([P, PASS], F32, name="bank2")
+            for a in range(H_PASSES):
+                nc.tensor.matmul_mx(
+                    out=bank[:, 0:width],
+                    lhsT=waw[a][g][:, 2 * t * P : 2 * (t + 1) * P].bitcast(FP4X4),
+                    lhsT_scale=was[a][g][:, t * P : (t + 1) * P],
+                    rhs=hc[half][a][:, c0 : c0 + width].bitcast(FP8X4),
+                    rhs_scale=hs[half][a][:, c0 : c0 + width],
+                    start=(a == 0),
+                    stop=(a == H_PASSES - 1),
+                )
+            if on_vector:
+                nc.vector.tensor_copy(e_sb[i][:, s0 : s0 + width], bank[:, 0:width])
+            else:
+                nc.scalar.copy(e_sb[i][:, s0 : s0 + width], bank[:, 0:width])
+
+        n_tiles = N_GROUPS * PACK
+        steps = [(0, 0), (1, 0), (0, 1), (1, 1), (0, 2), (1, 2)] + [(ci, b) for ci in (2, 3) for b in range(H_PASSES)]
+        quantize_w1(0)
+        for k, (ci, b) in enumerate(steps):
+            stage1(ci, b)
+            if k in (0, 2):
+                quantize_w1(k // 2 + 1)
+            if k > 0:
+                quantize_h(*steps[k - 1])
+        quantize_h(*steps[-1])
+        for ci in range(2):
+            for i in range(n_tiles):
+                stage2(i, ci * CHUNK, CHUNK, False)
+        for i in range(EARLY):
+            stage2(i, 2 * CHUNK, CHUNK, False)
+
+        out0_view = out_0.rearrange("(g p t) m -> g p t m", p=P, t=PACK)
+        y_sb = [keep.tile([P, PACK, M], F32, name=f"y{g}") for g in range(N_GROUPS)]
+        gate, picked, diff = {}, {}, {}
+        pieces = [(i, 0, M) for i in range(n_tiles - 1)] + [(n_tiles - 1, 0, M // 2), (n_tiles - 1, M // 2, M // 2)]
+
+        def look(k):
+            i, m0, width = pieces[k]
+            cols = slice(m0 // 16, (m0 + width) // 16)
+            gate[k] = ring.tile([P, width], F32, name="gate")
+            nc.scalar.activation(gate[k][:], e_sb[i][:].indirect(pos1_sb[:, cols]), ACT.Sigmoid, bias=limit_sb[:, i : i + 1])
+            picked[k] = ring.tile([P, width], F32, name="picked")
+            nc.vector.tensor_copy(picked[k][:], e_sb[i][:].indirect(pos2_sb[:, cols]))
+
+        def higher(k):
+            i, m0, width = pieces[k]
+            g, t = divmod(i, PACK)
+            nc.vector.tensor_tensor(picked[k][:], picked[k][:], clear_sb[g][:, t, m0 : m0 + width], ALU.max)
+
+        def combine(k):
+            i, m0, width = pieces[k]
+            g, t = divmod(i, PACK)
+            diff[k] = ring.tile([P, width], F32, name="diff")
+            nc.vector.tensor_tensor(diff[k][:], picked[k][:], gate[k][:], ALU.subtract)
+            nc.scalar.activation(y_sb[g][:, t, m0 : m0 + width], diff[k][:], ACT.Copy, scale=gain_sb[:, i : i + 1])
+            nc.sync.dma_start(out0_view[g][:, t, m0 : m0 + width], y_sb[g][:, t, m0 : m0 + width])
+
+        ybf = {}
+        ys = [keep.tile([P, M], U8, name=f"ys{g}", align_bytes=64) for g in range(N_GROUPS)]
+
+        def round_y(g, m0, width, copy):
+            ybf[(g, m0)] = keep.tile([P, PACK * width], BF16, name=f"ybf{g}_{m0}", align_bytes=64)
+            copy(
+                ybf[(g, m0)][:].rearrange("p (c i t) -> p c t i", i=4, t=PACK),
+                y_sb[g][:, :, m0 : m0 + width].rearrange("p t (c i) -> p c t i", i=4),
+            )
+
+        def planes(g, m0, width):
+            yc = keep.tile([P, width], I32, name=f"yc{g}_{m0}", align_bytes=64)
+            nc.vector.quantize_mx(out=yc[:].bitcast(FP8X4), scales=ys[g][:, m0 : m0 + width], in_=ybf[(g, m0)][:])
+            nc.sync.dma_start(out_1[g].rearrange("p m t -> p (m t)").bitcast(I32)[:, m0 : m0 + width], yc[:])
+
+        def store_scales(g, queues):
+            for q in range(4):
+                queues[q % len(queues)].dma_start(
+                    out_2[g, 4 * q : 4 * q + 4, :].bitcast(I32), ys[g][32 * q : 32 * q + 4, :].bitcast(I32)
+                )
+
+        for step in range(len(pieces) + 3):
+            if step < EARLY:
+                stage2(step, 3 * CHUNK, CHUNK, step == 0)
+            elif step < n_tiles:
+                stage2(step, 2 * CHUNK, 2 * CHUNK, False)
+            if 0 <= step - 1 < len(pieces):
+                look(step - 1)
+            if 0 <= step - 3 < len(pieces):
+                combine(step - 3)
+                if step - 3 == PACK - 1:
+                    round_y(0, 0, M, nc.scalar.copy)
+                if step - 3 == n_tiles - 1:
+                    round_y(1, 0, M // 2, nc.scalar.copy)
+            if 0 <= step - 2 < len(pieces):
+                higher(step - 2)
+            if step - 3 == PACK + 1:
+                planes(0, 0, M)
+                store_scales(0, [nc.sync])
+        planes(1, 0, M // 2)
+        round_y(1, M // 2, M // 2, nc.vector.tensor_copy)
+        planes(1, M // 2, M // 2)
+        store_scales(1, [nc.scalar, nc.sync])

@@ -23,7 +23,7 @@ H_PASSES = H // PASS
 N_GROUPS = N // PASS
 SUB = 128
 CHUNK = 256
-EARLY = 2
+AHEAD = (8, 4, 2)
 
 
 def tile_list_fog_hours_kernel(
@@ -32,6 +32,7 @@ def tile_list_fog_hours_kernel(
     nc = tc.nc
     with ExitStack() as ctx:
         keep = ctx.enter_context(tc.tile_pool(name="keep", bufs=1))
+        share = ctx.enter_context(tc.tile_pool(name="share", bufs=1))
         ring = ctx.enter_context(tc.tile_pool(name="ring", bufs=3))
         ps1 = ctx.enter_context(tc.psum_pool(name="ps1", bufs=4))
         ps2 = ctx.enter_context(tc.psum_pool(name="ps2", bufs=4))
@@ -39,89 +40,108 @@ def tile_list_fog_hours_kernel(
         offs_sb = keep.tile([P, S // 16], U16, name="offs_sb")
         pos1_sb = keep.tile([P, M // 16], U16, name="pos1_sb")
         pos2_sb = keep.tile([P, M // 16], U16, name="pos2_sb")
-        tabw = keep.tile([P, T], I32, name="tabw", align_bytes=64)
-        tabs = keep.tile([P, T], U8, name="tabs", align_bytes=64)
-        was_raw = keep.tile([P, H_PASSES * N], U8, name="was_raw", align_bytes=64)
-        nc.vector.memset(tabs[:].bitcast(I32), 0)
-        nc.gpsimd.memset(was_raw[:].bitcast(I32), 0)
+        KB = 1024
+        tabw = share.tile([P, T], I32, name="tabw", offset=0)
+        tabs = share.tile([P, T], U8, name="tabs", offset=30 * KB)
+        spread = keep.tile([P, S], U8, name="spread")
+        was_raw = keep.tile([P, H_PASSES * PASS], U8, name="was_raw")
+        was_dealt = keep.tile([P, H_PASSES * PASS], U8, name="was_dealt")
+        was_live = [keep.tile([P, H_PASSES * PASS], U8, name=f"was_live{g}", align_bytes=64) for g in range(N_GROUPS)]
+        vs = keep.tile([P, S], U8, name="vs", align_bytes=64)
+        low_sb = keep.tile([P, H_PASSES, PACK], F32, name="low_sb")
 
-        nc.sync.dma_start(tabw[:], tab_words[0].rearrange("p n t -> p (n t)").bitcast(I32))
-        nc.sync.dma_start(offs_sb[:], offs)
-        for q in range(4):
-            nc.sync.dma_start(tabs[32 * q : 32 * q + 4, :].bitcast(I32), tab_scales[0, 4 * q : 4 * q + 4, :].bitcast(I32))
+        nc.gpsimd.memset(tabs[:].bitcast(I32), 0)
+        nc.vector.memset(was_raw[:].bitcast(I32), 0)
+        nc.vector.memset(vs[:].bitcast(I32), 0)
+        for g in range(N_GROUPS):
+            nc.vector.memset(was_live[g][:].bitcast(I32), 0)
 
         w1_view = w1.rearrange("(p j) c -> p j c", j=PACK)
-        w1_parts = []
-        for b in range(H_PASSES):
-            cuts = (0, 256, 384, PASS) if b == 0 else (0, PASS)
-            parts = []
-            for c0, c1 in zip(cuts[:-1], cuts[1:]):
-                raw = keep.tile([P, PACK, c1 - c0], F32, name=f"w1raw{b}_{c0}")
-                nc.sync.dma_start(raw[:], w1_view[:, :, b * PASS + c0 : b * PASS + c1])
-                parts.append((c0, c1, raw))
-            w1_parts.append(parts)
-            if b == 1:
-                for q in range(4):
-                    nc.sync.dma_start(
-                        was_raw[32 * q : 32 * q + 4, :].bitcast(I32).rearrange("r (a c) -> r a c", a=H_PASSES),
-                        wa_scales[:, 4 * q : 4 * q + 4, :].bitcast(I32).rearrange("a r c -> r a c"),
-                    )
+        w1_parts = [[], [], []]
 
-        low_sb = keep.tile([P, H_PASSES, PACK], F32, name="low_sb")
-        limit_sb = keep.tile([P, N_GROUPS * PACK], F32, name="limit_sb")
-        gain_sb = keep.tile([P, N_GROUPS * PACK], F32, name="gain_sb")
-        nc.gpsimd.dma_start(low_sb[:], low.rearrange("(b p t) -> p b t", p=P, t=PACK))
-        nc.gpsimd.dma_start(limit_sb[:].rearrange("p (g t) -> p g t", t=PACK), limit.rearrange("(g p t) -> p g t", p=P, t=PACK))
-        nc.gpsimd.dma_start(gain_sb[:].rearrange("p (g t) -> p g t", t=PACK), gain.rearrange("(g p t) -> p g t", p=P, t=PACK))
+        def load_w1(b, c0, c1, offset):
+            raw = share.tile([P, PACK, c1 - c0], F32, name=f"w1raw{b}_{c0}", offset=offset)
+            nc.sync.dma_start(raw[:], w1_view[:, :, b * PASS + c0 : b * PASS + c1])
+            w1_parts[b].append((c0, c1, raw))
+
+        nc.sync.dma_start(offs_sb[:], offs)
+        nc.sync.dma_start(pos1_sb[:], pos1)
+        nc.sync.dma_start(pos2_sb[:], pos2)
+        load_w1(0, 0, PASS // 2, 16 * KB)
+        load_w1(0, PASS // 2, PASS, 20 * KB)
+        nc.sync.dma_start(low_sb[:], low.rearrange("(b p t) -> p b t", p=P, t=PACK))
+        nc.sync.dma_start(tabs[0:P:8, :].bitcast(I32), tab_scales[0].bitcast(I32))
+        nc.sync.dma_start(
+            was_raw[0:P:4, :].bitcast(I32).rearrange("r (a c) -> r a c", a=H_PASSES),
+            wa_scales.bitcast(I32).rearrange("a q (g c) -> (q g) a c", g=N_GROUPS),
+        )
+        nc.sync.dma_start(tabw[:], tab_words[0].rearrange("p n t -> p (n t)").bitcast(I32))
+
+        nc.vector.tensor_copy(spread[:], tabs[:].indirect(offs_sb[:]))
+        for q in range(4):
+            nc.sync.dma_start(vs[32 * q : 32 * q + 4, :].bitcast(I32), spread[32 * q : 32 * q + 32 : 8, :].bitcast(I32))
+
+        w1c, w1s, w1bf = [], [], []
+        for b in range(H_PASSES):
+            w1bf.append(keep.tile([P, PACK * PASS], BF16, name=f"w1bf{b}", align_bytes=64))
+            w1c.append(keep.tile([P, PASS], U32, name=f"w1c{b}", align_bytes=64))
+            w1s.append(keep.tile([P, PASS], U8, name=f"w1s{b}", align_bytes=64))
+
+        def round_w1(b):
+            dealt = w1bf[b][:].rearrange("p (t m j) -> p m j t", t=PACK, j=PACK)
+            for c0, c1, raw in w1_parts[b]:
+                nc.scalar.copy(dealt[:, c0 // PACK : c1 // PACK, :, :], raw[:].rearrange("p j (m t) -> p m j t", t=PACK))
+
+        def quantize_w1(b):
+            nc.vector.quantize_mx(out=w1c[b][:].bitcast(FP8X4), scales=w1s[b][:], in_=w1bf[b][:])
+
+        load_w1(1, 0, PASS, 24 * KB)
+        load_w1(2, 0, PASS, 32 * KB)
+
+        round_w1(0)
+        quantize_w1(0)
+        nc.vector.tensor_copy(
+            was_dealt[:].rearrange("p (a t q) -> p a t q", a=H_PASSES, t=PACK),
+            was_raw[:].rearrange("p (a q t) -> p a t q", a=H_PASSES, t=PACK),
+        )
+        for g in range(N_GROUPS):
+            for q in range(4):
+                (nc.sync, nc.gpsimd)[g].dma_start(
+                    was_live[g][32 * q : 32 * q + 4, :].bitcast(I32),
+                    was_dealt[32 * q + 4 * g : 32 * q + 32 : 8, :].bitcast(I32),
+                )
+        was = [[was_live[g][:, a * PASS : (a + 1) * PASS] for g in range(N_GROUPS)] for a in range(H_PASSES)]
+
+        vw = []
+        for ci in range(S // CHUNK):
+            cols = offs_sb[:, ci * CHUNK // 16 : (ci + 1) * CHUNK // 16]
+            wt = keep.tile([P, CHUNK], U32, name=f"vw{ci}", align_bytes=64)
+            nc.vector.tensor_copy(wt[:], tabw[:].bitcast(U32).indirect(cols))
+            vw.append(wt)
+
+        round_w1(1)
+        round_w1(2)
 
         waw_raw = []
         for g in range(N_GROUPS):
-            raw = keep.tile([P, H_PASSES * PASS // 2], I32, name=f"waw_raw{g}")
+            raw = share.tile([P, H_PASSES * PASS // 2], I32, name=f"waw_raw{g}", offset=3 * KB * g)
             nc.sync.dma_start(
                 raw[:].rearrange("p (a c) -> p a c", a=H_PASSES),
                 wa_words[:, :, 2 * g * PASS : 2 * (g + 1) * PASS].bitcast(I32).rearrange("a p c -> p a c"),
             )
             waw_raw.append(raw)
-        nc.sync.dma_start(pos1_sb[:], pos1)
-        nc.sync.dma_start(pos2_sb[:], pos2)
         clear_view = clear.rearrange("(g p t) m -> g p t m", p=P, t=PACK)
         clear_sb = []
         for g in range(N_GROUPS):
-            ct = keep.tile([P, PACK, M], F32, name=f"clear{g}")
+            ct = share.tile([P, PACK, M], F32, name=f"clear{g}", offset=(8, 24)[g] * KB)
             nc.sync.dma_start(ct[:], clear_view[g])
             clear_sb.append(ct)
-
-        vw, vs = [], []
-        for half in range(2):
-            cols = offs_sb[:, half * 32 : (half + 1) * 32]
-            wt = keep.tile([P, S // 2], U32, name=f"vw{half}", align_bytes=64)
-            st = keep.tile([P, S // 2], U8, name=f"vs{half}", align_bytes=64)
-            nc.vector.tensor_copy(wt[:], tabw[:].bitcast(U32).indirect(cols))
-            nc.vector.tensor_copy(st[:], tabs[:].indirect(cols))
-            vw.append(wt)
-            vs.append(st)
-
-        w1c, w1s, w1bf = [], [], []
-        for b in range(H_PASSES):
-            bf = keep.tile([P, PACK * PASS], BF16, name=f"w1bf{b}", align_bytes=64)
-            dealt = bf[:].rearrange("p (t m j) -> p m j t", t=PACK, j=PACK)
-            for c0, c1, raw in w1_parts[b]:
-                nc.scalar.copy(dealt[:, c0 // PACK : c1 // PACK, :, :], raw[:].rearrange("p j (m t) -> p m j t", t=PACK))
-            w1bf.append(bf)
-            w1c.append(keep.tile([P, PASS], U32, name=f"w1c{b}", align_bytes=64))
-            w1s.append(keep.tile([P, PASS], U8, name=f"w1s{b}", align_bytes=64))
-
-        def quantize_w1(b):
-            nc.vector.quantize_mx(out=w1c[b][:].bitcast(FP8X4), scales=w1s[b][:], in_=w1bf[b][:])
+        limit_sb = share.tile([P, N_GROUPS * PACK], F32, name="limit_sb", offset=32 * KB)
+        gain_sb = share.tile([P, N_GROUPS * PACK], F32, name="gain_sb", offset=32 * KB + 64)
+        nc.sync.dma_start(limit_sb[:].rearrange("p (g t) -> p g t", t=PACK), limit.rearrange("(g p t) -> p g t", p=P, t=PACK))
+        nc.sync.dma_start(gain_sb[:].rearrange("p (g t) -> p g t", t=PACK), gain.rearrange("(g p t) -> p g t", p=P, t=PACK))
 
         waw = [[None] * N_GROUPS for a in range(H_PASSES)]
-        was = [[None] * N_GROUPS for a in range(H_PASSES)]
-        for g in range(N_GROUPS):
-            for a in range(H_PASSES):
-                st = keep.tile([P, PASS], U8, name=f"was{a}_{g}", align_bytes=64)
-                src = was_raw[:, a * N + g * PASS : a * N + (g + 1) * PASS]
-                nc.gpsimd.tensor_copy(st[:].rearrange("p (t q) -> p t q", t=PACK), src.rearrange("p (q t) -> p t q", t=PACK))
-                was[a][g] = st
         for g in range(N_GROUPS):
             wt = keep.tile([P, H_PASSES * 2 * PASS], U8, name=f"waw{g}", align_bytes=64)
             nc.scalar.copy(
@@ -141,15 +161,14 @@ def tile_list_fog_hours_kernel(
             hbf[(ci, b)] = bf
             for u in range(CHUNK // SUB):
                 col = ci * CHUNK + u * SUB
-                half, c0 = divmod(col, S // 2)
                 bank = ps1.tile([P, PACK, SUB], F32, name="bank1")
                 for t in range(PACK):
                     nc.tensor.matmul_mx(
                         out=bank[:, t, :],
                         lhsT=w1c[b][:, t * P : (t + 1) * P].bitcast(FP8X4),
                         lhsT_scale=w1s[b][:, t * P : (t + 1) * P],
-                        rhs=vw[half][:, c0 : c0 + SUB].bitcast(FP8X4),
-                        rhs_scale=vs[half][:, c0 : c0 + SUB],
+                        rhs=vw[ci][:, u * SUB : (u + 1) * SUB].bitcast(FP8X4),
+                        rhs_scale=vs[:, col : col + SUB],
                         start=True,
                         stop=True,
                     )
@@ -186,46 +205,49 @@ def tile_list_fog_hours_kernel(
                 nc.scalar.copy(e_sb[i][:, s0 : s0 + width], bank[:, 0:width])
 
         n_tiles = N_GROUPS * PACK
-        steps = [(0, 0), (1, 0), (0, 1), (1, 1), (0, 2), (1, 2)] + [(ci, b) for ci in (2, 3) for b in range(H_PASSES)]
-        quantize_w1(0)
+        steps = [(0, 0), (1, 0), (0, 1), (0, 2), (1, 1), (1, 2)] + [(ci, b) for ci in (2, 3) for b in range(H_PASSES)]
         for k, (ci, b) in enumerate(steps):
             stage1(ci, b)
-            if k in (0, 2):
-                quantize_w1(k // 2 + 1)
+            if k in (1, 2):
+                quantize_w1(k)
             if k > 0:
                 quantize_h(*steps[k - 1])
         quantize_h(*steps[-1])
-        for ci in range(2):
-            for i in range(n_tiles):
+        for ci, ahead in enumerate(AHEAD):
+            for i in range(ahead):
                 stage2(i, ci * CHUNK, CHUNK, False)
-        for i in range(EARLY):
-            stage2(i, 2 * CHUNK, CHUNK, False)
 
         out0_view = out_0.rearrange("(g p t) m -> g p t m", p=P, t=PACK)
         y_sb = [keep.tile([P, PACK, M], F32, name=f"y{g}") for g in range(N_GROUPS)]
         gate, picked, diff = {}, {}, {}
-        pieces = [(i, 0, M) for i in range(n_tiles - 1)] + [(n_tiles - 1, 0, M // 2), (n_tiles - 1, M // 2, M // 2)]
+        pieces = [(i, 2, 0, M) for i in range(0, n_tiles - 2, 2)]
+        pieces = pieces + [(n_tiles - 2, 1, 0, M), (n_tiles - 1, 1, 0, M // 2), (n_tiles - 1, 1, M // 2, M // 2)]
 
         def look(k):
-            i, m0, width = pieces[k]
+            i0, count, m0, width = pieces[k]
             cols = slice(m0 // 16, (m0 + width) // 16)
-            gate[k] = ring.tile([P, width], F32, name="gate")
-            nc.scalar.activation(gate[k][:], e_sb[i][:].indirect(pos1_sb[:, cols]), ACT.Sigmoid, bias=limit_sb[:, i : i + 1])
-            picked[k] = ring.tile([P, width], F32, name="picked")
-            nc.vector.tensor_copy(picked[k][:], e_sb[i][:].indirect(pos2_sb[:, cols]))
+            gate[k] = ring.tile([P, count, width], F32, name="gate")
+            picked[k] = ring.tile([P, count, width], F32, name="picked")
+            for u in range(count):
+                i = i0 + u
+                nc.scalar.activation(gate[k][:, u, :], e_sb[i][:].indirect(pos1_sb[:, cols]), ACT.Sigmoid, bias=limit_sb[:, i : i + 1])
+                nc.vector.tensor_copy(picked[k][:, u, :], e_sb[i][:].indirect(pos2_sb[:, cols]))
 
         def higher(k):
-            i, m0, width = pieces[k]
-            g, t = divmod(i, PACK)
-            nc.vector.tensor_tensor(picked[k][:], picked[k][:], clear_sb[g][:, t, m0 : m0 + width], ALU.max)
+            i0, count, m0, width = pieces[k]
+            g, t = divmod(i0, PACK)
+            nc.vector.tensor_tensor(picked[k][:], picked[k][:], clear_sb[g][:, t : t + count, m0 : m0 + width], ALU.max)
 
         def combine(k):
-            i, m0, width = pieces[k]
-            g, t = divmod(i, PACK)
-            diff[k] = ring.tile([P, width], F32, name="diff")
+            i0, count, m0, width = pieces[k]
+            g, t = divmod(i0, PACK)
+            diff[k] = ring.tile([P, count, width], F32, name="diff")
             nc.vector.tensor_tensor(diff[k][:], picked[k][:], gate[k][:], ALU.subtract)
-            nc.scalar.activation(y_sb[g][:, t, m0 : m0 + width], diff[k][:], ACT.Copy, scale=gain_sb[:, i : i + 1])
-            nc.sync.dma_start(out0_view[g][:, t, m0 : m0 + width], y_sb[g][:, t, m0 : m0 + width])
+            for u in range(count):
+                nc.scalar.activation(
+                    y_sb[g][:, t + u, m0 : m0 + width], diff[k][:, u, :], ACT.Copy, scale=gain_sb[:, i0 + u : i0 + u + 1]
+                )
+            nc.sync.dma_start(out0_view[g][:, t : t + count, m0 : m0 + width], y_sb[g][:, t : t + count, m0 : m0 + width])
 
         ybf = {}
         ys = [keep.tile([P, M], U8, name=f"ys{g}", align_bytes=64) for g in range(N_GROUPS)]
@@ -248,24 +270,35 @@ def tile_list_fog_hours_kernel(
                     out_2[g, 4 * q : 4 * q + 4, :].bitcast(I32), ys[g][32 * q : 32 * q + 4, :].bitcast(I32)
                 )
 
-        for step in range(len(pieces) + 3):
-            if step < EARLY:
-                stage2(step, 3 * CHUNK, CHUNK, step == 0)
-            elif step < n_tiles:
-                stage2(step, 2 * CHUNK, 2 * CHUNK, False)
-            if 0 <= step - 1 < len(pieces):
-                look(step - 1)
-            if 0 <= step - 3 < len(pieces):
-                combine(step - 3)
-                if step - 3 == PACK - 1:
-                    round_y(0, 0, M, nc.scalar.copy)
-                if step - 3 == n_tiles - 1:
-                    round_y(1, 0, M // 2, nc.scalar.copy)
-            if 0 <= step - 2 < len(pieces):
-                higher(step - 2)
-            if step - 3 == PACK + 1:
+        def finish_rows(k):
+            i0, count, m0, width = pieces[k]
+            for i in range(i0, i0 + count):
+                if m0 > 0:
+                    continue
+                if i >= AHEAD[1]:
+                    stage2(i, CHUNK, CHUNK, False)
+                if i >= AHEAD[2]:
+                    stage2(i, 2 * CHUNK, 2 * CHUNK, False)
+                else:
+                    stage2(i, 3 * CHUNK, CHUNK, i == 0)
+
+        finish_rows(0)
+        for k in range(len(pieces) + 1):
+            if k + 1 < len(pieces):
+                finish_rows(k + 1)
+            if k < len(pieces):
+                look(k)
+            if k >= 1:
+                combine(k - 1)
+            if k < len(pieces):
+                higher(k)
+            if k - 1 == 1:
+                round_y(0, 0, M, nc.vector.tensor_copy)
+            if k - 1 == 2:
                 planes(0, 0, M)
                 store_scales(0, [nc.sync])
+            if k - 1 == len(pieces) - 2:
+                round_y(1, 0, M // 2, nc.scalar.copy)
         planes(1, 0, M // 2)
         round_y(1, M // 2, M // 2, nc.vector.tensor_copy)
         planes(1, M // 2, M // 2)

@@ -242,7 +242,8 @@ def tile_list_fog_hours_kernel(
             i0, count, m0, width = pieces[k]
             g, t = divmod(i0, PACK)
             diff[k] = ring.tile([P, count, width], F32, name="diff")
-            nc.vector.tensor_tensor(diff[k][:], picked[k][:], gate[k][:], ALU.subtract)
+            engine = nc.gpsimd if width == M else nc.vector
+            engine.tensor_tensor(diff[k][:], picked[k][:], gate[k][:], ALU.subtract)
             for u in range(count):
                 nc.scalar.activation(
                     y_sb[g][:, t + u, m0 : m0 + width], diff[k][:, u, :], ACT.Copy, scale=gain_sb[:, i0 + u : i0 + u + 1]
@@ -276,7 +277,7 @@ def tile_list_fog_hours_kernel(
                 if m0 > 0:
                     continue
                 if i >= AHEAD[1]:
-                    stage2(i, CHUNK, CHUNK, False)
+                    stage2(i, CHUNK, CHUNK, True)
                 if i >= AHEAD[2]:
                     stage2(i, 2 * CHUNK, 2 * CHUNK, False)
                 else:

@@ -19,11 +19,23 @@ ACT = mybir.ActivationFunctionType
 P = 128
 PACK = 4
 PASS = P * PACK
+QUADRANTS = 4
+LIST_ROWS = 16
 H_PASSES = H // PASS
 N_GROUPS = N // PASS
+ROW_TILES = N_GROUPS * PACK
 SUB = 128
 CHUNK = 256
 AHEAD = (8, 4, 2)
+ZERO_SPLIT = 2560
+
+KB = 1024
+AT_TABLE_WORDS = 0
+AT_WA_WORDS = (0, 3 * KB)
+AT_W1 = (16 * KB, 24 * KB, 32 * KB)
+AT_TABLE_SCALES = 30 * KB
+AT_CLEAR = (8 * KB, 24 * KB)
+AT_LIMIT, AT_GAIN = 32 * KB, 32 * KB + 64
 
 
 def tile_list_fog_hours_kernel(
@@ -37,143 +49,148 @@ def tile_list_fog_hours_kernel(
         ps1 = ctx.enter_context(tc.psum_pool(name="ps1", bufs=4))
         ps2 = ctx.enter_context(tc.psum_pool(name="ps2", bufs=4))
 
-        offs_sb = keep.tile([P, S // 16], U16, name="offs_sb")
-        pos1_sb = keep.tile([P, M // 16], U16, name="pos1_sb")
-        pos2_sb = keep.tile([P, M // 16], U16, name="pos2_sb")
-        KB = 1024
-        tabw = share.tile([P, T], I32, name="tabw", offset=0)
-        tabs = share.tile([P, T], U8, name="tabs", offset=30 * KB)
-        spread = keep.tile([P, S], U8, name="spread")
-        was_raw = keep.tile([P, H_PASSES * PASS], U8, name="was_raw")
-        was_dealt = keep.tile([P, H_PASSES * PASS], U8, name="was_dealt")
-        was_live = [keep.tile([P, H_PASSES * PASS], U8, name=f"was_live{g}", align_bytes=64) for g in range(N_GROUPS)]
-        vs = keep.tile([P, S], U8, name="vs", align_bytes=64)
+        offs_sb = keep.tile([P, S // LIST_ROWS], U16, name="offs_sb")
+        pos1_sb = keep.tile([P, M // LIST_ROWS], U16, name="pos1_sb")
+        pos2_sb = keep.tile([P, M // LIST_ROWS], U16, name="pos2_sb")
+        table_words = share.tile([P, T], I32, name="table_words", offset=AT_TABLE_WORDS)
+        table_scales = share.tile([P, T], U8, name="table_scales", offset=AT_TABLE_SCALES)
+        picked_scales = keep.tile([P, S], U8, name="picked_scales")
+        wa_scales_raw = keep.tile([P, H_PASSES * PASS], U8, name="wa_scales_raw")
+        wa_scales_dealt = keep.tile([P, H_PASSES * PASS], U8, name="wa_scales_dealt")
+        wa_scale_tiles = [keep.tile([P, H_PASSES * PASS], U8, name=f"wa_scale_tile{g}", align_bytes=64) for g in range(N_GROUPS)]
+        v_scales = keep.tile([P, S], U8, name="v_scales", align_bytes=64)
         low_sb = keep.tile([P, H_PASSES, PACK], F32, name="low_sb")
 
-        nc.gpsimd.memset(tabs[:].bitcast(I32), 0)
-        nc.vector.memset(was_raw[:].bitcast(I32), 0)
-        nc.vector.memset(vs[:].bitcast(I32), 0)
+        nc.gpsimd.memset(table_scales[:, 0:ZERO_SPLIT].bitcast(I32), 0)
+        nc.vector.memset(table_scales[:, ZERO_SPLIT:T].bitcast(I32), 0)
+        nc.vector.memset(wa_scales_raw[:].bitcast(I32), 0)
+        nc.vector.memset(v_scales[:].bitcast(I32), 0)
         for g in range(N_GROUPS):
-            nc.vector.memset(was_live[g][:].bitcast(I32), 0)
+            nc.vector.memset(wa_scale_tiles[g][:].bitcast(I32), 0)
 
         w1_view = w1.rearrange("(p j) c -> p j c", j=PACK)
-        w1_parts = [[], [], []]
+        w1_parts = [[] for b in range(H_PASSES)]
 
-        def load_w1(b, c0, c1, offset):
-            raw = share.tile([P, PACK, c1 - c0], F32, name=f"w1raw{b}_{c0}", offset=offset)
+        def load_w1(b, c0, c1):
+            raw = share.tile([P, PACK, c1 - c0], F32, name=f"w1_raw{b}_{c0}", offset=AT_W1[b] + 4 * PACK * c0)
             nc.sync.dma_start(raw[:], w1_view[:, :, b * PASS + c0 : b * PASS + c1])
             w1_parts[b].append((c0, c1, raw))
 
         nc.sync.dma_start(offs_sb[:], offs)
+        load_w1(0, 0, PASS // 2)
+        load_w1(0, PASS // 2, PASS)
         nc.sync.dma_start(pos1_sb[:], pos1)
-        nc.sync.dma_start(pos2_sb[:], pos2)
-        load_w1(0, 0, PASS // 2, 16 * KB)
-        load_w1(0, PASS // 2, PASS, 20 * KB)
-        nc.sync.dma_start(low_sb[:], low.rearrange("(b p t) -> p b t", p=P, t=PACK))
-        nc.sync.dma_start(tabs[0:P:8, :].bitcast(I32), tab_scales[0].bitcast(I32))
+        nc.sync.dma_start(table_scales[0:P:8, :].bitcast(I32), tab_scales[0].bitcast(I32))
         nc.sync.dma_start(
-            was_raw[0:P:4, :].bitcast(I32).rearrange("r (a c) -> r a c", a=H_PASSES),
+            wa_scales_raw[0:P:4, :].bitcast(I32).rearrange("r (a c) -> r a c", a=H_PASSES),
             wa_scales.bitcast(I32).rearrange("a q (g c) -> (q g) a c", g=N_GROUPS),
         )
-        nc.sync.dma_start(tabw[:], tab_words[0].rearrange("p n t -> p (n t)").bitcast(I32))
+        nc.sync.dma_start(table_words[:], tab_words[0].rearrange("p n t -> p (n t)").bitcast(I32))
+        nc.sync.dma_start(low_sb[:], low.rearrange("(b p t) -> p b t", p=P, t=PACK))
+        nc.sync.dma_start(pos2_sb[:], pos2)
 
-        nc.vector.tensor_copy(spread[:], tabs[:].indirect(offs_sb[:]))
-        for q in range(4):
-            nc.sync.dma_start(vs[32 * q : 32 * q + 4, :].bitcast(I32), spread[32 * q : 32 * q + 32 : 8, :].bitcast(I32))
+        nc.vector.tensor_copy(picked_scales[:], table_scales[:].indirect(offs_sb[:]))
+        for quad in range(QUADRANTS):
+            nc.sync.dma_start(
+                v_scales[32 * quad : 32 * quad + 4, :].bitcast(I32),
+                picked_scales[32 * quad : 32 * quad + 32 : 8, :].bitcast(I32),
+            )
 
-        w1c, w1s, w1bf = [], [], []
+        w1_codes, w1_scales, w1_bf = [], [], []
         for b in range(H_PASSES):
-            w1bf.append(keep.tile([P, PACK * PASS], BF16, name=f"w1bf{b}", align_bytes=64))
-            w1c.append(keep.tile([P, PASS], U32, name=f"w1c{b}", align_bytes=64))
-            w1s.append(keep.tile([P, PASS], U8, name=f"w1s{b}", align_bytes=64))
+            w1_bf.append(keep.tile([P, PACK * PASS], BF16, name=f"w1_bf{b}", align_bytes=64))
+            w1_codes.append(keep.tile([P, PASS], U32, name=f"w1_codes{b}", align_bytes=64))
+            w1_scales.append(keep.tile([P, PASS], U8, name=f"w1_scales{b}", align_bytes=64))
 
         def round_w1(b):
-            dealt = w1bf[b][:].rearrange("p (t m j) -> p m j t", t=PACK, j=PACK)
+            dealt = w1_bf[b][:].rearrange("p (t m j) -> p m j t", t=PACK, j=PACK)
             for c0, c1, raw in w1_parts[b]:
                 nc.scalar.copy(dealt[:, c0 // PACK : c1 // PACK, :, :], raw[:].rearrange("p j (m t) -> p m j t", t=PACK))
 
         def quantize_w1(b):
-            nc.vector.quantize_mx(out=w1c[b][:].bitcast(FP8X4), scales=w1s[b][:], in_=w1bf[b][:])
+            nc.vector.quantize_mx(out=w1_codes[b][:].bitcast(FP8X4), scales=w1_scales[b][:], in_=w1_bf[b][:])
 
-        load_w1(1, 0, PASS, 24 * KB)
-        load_w1(2, 0, PASS, 32 * KB)
+        for b in range(1, H_PASSES):
+            load_w1(b, 0, PASS)
 
         round_w1(0)
         quantize_w1(0)
+
         nc.vector.tensor_copy(
-            was_dealt[:].rearrange("p (a t q) -> p a t q", a=H_PASSES, t=PACK),
-            was_raw[:].rearrange("p (a q t) -> p a t q", a=H_PASSES, t=PACK),
+            wa_scales_dealt[:].rearrange("p (a t m) -> p a t m", a=H_PASSES, t=PACK),
+            wa_scales_raw[:].rearrange("p (a m t) -> p a t m", a=H_PASSES, t=PACK),
         )
-        for g in range(N_GROUPS):
-            for q in range(4):
-                (nc.sync, nc.gpsimd)[g].dma_start(
-                    was_live[g][32 * q : 32 * q + 4, :].bitcast(I32),
-                    was_dealt[32 * q + 4 * g : 32 * q + 32 : 8, :].bitcast(I32),
+        for g, queue in enumerate((nc.sync, nc.gpsimd)):
+            for quad in range(QUADRANTS):
+                queue.dma_start(
+                    wa_scale_tiles[g][32 * quad : 32 * quad + 4, :].bitcast(I32),
+                    wa_scales_dealt[32 * quad + 4 * g : 32 * quad + 32 : 8, :].bitcast(I32),
                 )
-        was = [[was_live[g][:, a * PASS : (a + 1) * PASS] for g in range(N_GROUPS)] for a in range(H_PASSES)]
 
-        vw = []
+        v_words = []
         for ci in range(S // CHUNK):
-            cols = offs_sb[:, ci * CHUNK // 16 : (ci + 1) * CHUNK // 16]
-            wt = keep.tile([P, CHUNK], U32, name=f"vw{ci}", align_bytes=64)
-            nc.vector.tensor_copy(wt[:], tabw[:].bitcast(U32).indirect(cols))
-            vw.append(wt)
+            entries = offs_sb[:, ci * CHUNK // LIST_ROWS : (ci + 1) * CHUNK // LIST_ROWS]
+            words = keep.tile([P, CHUNK], U32, name=f"v_words{ci}", align_bytes=64)
+            nc.vector.tensor_copy(words[:], table_words[:].bitcast(U32).indirect(entries))
+            v_words.append(words)
 
-        round_w1(1)
-        round_w1(2)
+        for b in range(1, H_PASSES):
+            round_w1(b)
 
-        waw_raw = []
+        wa_words_raw = []
         for g in range(N_GROUPS):
-            raw = share.tile([P, H_PASSES * PASS // 2], I32, name=f"waw_raw{g}", offset=3 * KB * g)
+            raw = share.tile([P, H_PASSES * PASS // 2], I32, name=f"wa_words_raw{g}", offset=AT_WA_WORDS[g])
             nc.sync.dma_start(
                 raw[:].rearrange("p (a c) -> p a c", a=H_PASSES),
                 wa_words[:, :, 2 * g * PASS : 2 * (g + 1) * PASS].bitcast(I32).rearrange("a p c -> p a c"),
             )
-            waw_raw.append(raw)
+            wa_words_raw.append(raw)
         clear_view = clear.rearrange("(g p t) m -> g p t m", p=P, t=PACK)
         clear_sb = []
         for g in range(N_GROUPS):
-            ct = share.tile([P, PACK, M], F32, name=f"clear{g}", offset=(8, 24)[g] * KB)
-            nc.sync.dma_start(ct[:], clear_view[g])
-            clear_sb.append(ct)
-        limit_sb = share.tile([P, N_GROUPS * PACK], F32, name="limit_sb", offset=32 * KB)
-        gain_sb = share.tile([P, N_GROUPS * PACK], F32, name="gain_sb", offset=32 * KB + 64)
+            rows = share.tile([P, PACK, M], F32, name=f"clear{g}", offset=AT_CLEAR[g])
+            nc.sync.dma_start(rows[:], clear_view[g])
+            clear_sb.append(rows)
+        limit_sb = share.tile([P, ROW_TILES], F32, name="limit_sb", offset=AT_LIMIT)
+        gain_sb = share.tile([P, ROW_TILES], F32, name="gain_sb", offset=AT_GAIN)
         nc.sync.dma_start(limit_sb[:].rearrange("p (g t) -> p g t", t=PACK), limit.rearrange("(g p t) -> p g t", p=P, t=PACK))
         nc.sync.dma_start(gain_sb[:].rearrange("p (g t) -> p g t", t=PACK), gain.rearrange("(g p t) -> p g t", p=P, t=PACK))
 
-        waw = [[None] * N_GROUPS for a in range(H_PASSES)]
+        wa_word_tiles = []
         for g in range(N_GROUPS):
-            wt = keep.tile([P, H_PASSES * 2 * PASS], U8, name=f"waw{g}", align_bytes=64)
+            dealt_words = keep.tile([P, H_PASSES * 2 * PASS], U8, name=f"wa_word_tile{g}", align_bytes=64)
             nc.scalar.copy(
-                wt[:].bitcast(U16).rearrange("p (a t q) -> p a t q", a=H_PASSES, t=PACK),
-                waw_raw[g][:].bitcast(U16).rearrange("p (a q t) -> p a t q", a=H_PASSES, t=PACK),
+                dealt_words[:].bitcast(U16).rearrange("p (a t m) -> p a t m", a=H_PASSES, t=PACK),
+                wa_words_raw[g][:].bitcast(U16).rearrange("p (a m t) -> p a t m", a=H_PASSES, t=PACK),
             )
-            for a in range(H_PASSES):
-                waw[a][g] = wt[:, 2 * a * PASS : 2 * (a + 1) * PASS]
+            wa_word_tiles.append(dealt_words)
 
-        e_sb = [keep.tile([P, S], F32, name=f"e{i}") for i in range(N_GROUPS * PACK)]
-        hc = [[keep.tile([P, S // 2], U32, name=f"hc{half}_{b}", align_bytes=64) for b in range(H_PASSES)] for half in range(2)]
-        hs = [[keep.tile([P, S // 2], U8, name=f"hs{half}_{b}", align_bytes=64) for b in range(H_PASSES)] for half in range(2)]
-        hbf = {}
+        e_sb = [keep.tile([P, S], F32, name=f"e{i}") for i in range(ROW_TILES)]
+        h_codes = [
+            [keep.tile([P, S // 2], U32, name=f"h_codes{half}_{b}", align_bytes=64) for b in range(H_PASSES)] for half in range(2)
+        ]
+        h_scales = [
+            [keep.tile([P, S // 2], U8, name=f"h_scales{half}_{b}", align_bytes=64) for b in range(H_PASSES)] for half in range(2)
+        ]
+        h_bf = {}
 
         def stage1(ci, b):
-            bf = ring.tile([P, PACK * CHUNK], BF16, name="hbf", align_bytes=64)
-            hbf[(ci, b)] = bf
+            h_bf[(ci, b)] = ring.tile([P, PACK * CHUNK], BF16, name="h_bf", align_bytes=64)
             for u in range(CHUNK // SUB):
                 col = ci * CHUNK + u * SUB
                 bank = ps1.tile([P, PACK, SUB], F32, name="bank1")
                 for t in range(PACK):
                     nc.tensor.matmul_mx(
                         out=bank[:, t, :],
-                        lhsT=w1c[b][:, t * P : (t + 1) * P].bitcast(FP8X4),
-                        lhsT_scale=w1s[b][:, t * P : (t + 1) * P],
-                        rhs=vw[ci][:, u * SUB : (u + 1) * SUB].bitcast(FP8X4),
-                        rhs_scale=vs[:, col : col + SUB],
+                        lhsT=w1_codes[b][:, t * P : (t + 1) * P].bitcast(FP8X4),
+                        lhsT_scale=w1_scales[b][:, t * P : (t + 1) * P],
+                        rhs=v_words[ci][:, u * SUB : (u + 1) * SUB].bitcast(FP8X4),
+                        rhs_scale=v_scales[:, col : col + SUB],
                         start=True,
                         stop=True,
                     )
                 nc.vector.tensor_tensor(
-                    bf[:, u * PACK * SUB : (u + 1) * PACK * SUB].rearrange("p (j t) -> p j t", t=PACK),
+                    h_bf[(ci, b)][:, u * PACK * SUB : (u + 1) * PACK * SUB].rearrange("p (j t) -> p j t", t=PACK),
                     bank[:].rearrange("p t j -> p j t"),
                     low_sb[:, b : b + 1, :].to_broadcast([P, SUB, PACK]),
                     ALU.max,
@@ -182,50 +199,51 @@ def tile_list_fog_hours_kernel(
         def quantize_h(ci, b):
             half, c0 = divmod(ci * CHUNK, S // 2)
             nc.vector.quantize_mx(
-                out=hc[half][b][:, c0 : c0 + CHUNK].bitcast(FP8X4), scales=hs[half][b][:, c0 : c0 + CHUNK], in_=hbf[(ci, b)][:]
+                out=h_codes[half][b][:, c0 : c0 + CHUNK].bitcast(FP8X4),
+                scales=h_scales[half][b][:, c0 : c0 + CHUNK],
+                in_=h_bf[(ci, b)][:],
             )
 
-        def stage2(i, s0, width, on_vector):
+        def stage2(i, s0, width, copy_out):
             half, c0 = divmod(s0, S // 2)
             g, t = divmod(i, PACK)
             bank = ps2.tile([P, PASS], F32, name="bank2")
             for a in range(H_PASSES):
+                place = a * PASS + t * P
                 nc.tensor.matmul_mx(
                     out=bank[:, 0:width],
-                    lhsT=waw[a][g][:, 2 * t * P : 2 * (t + 1) * P].bitcast(FP4X4),
-                    lhsT_scale=was[a][g][:, t * P : (t + 1) * P],
-                    rhs=hc[half][a][:, c0 : c0 + width].bitcast(FP8X4),
-                    rhs_scale=hs[half][a][:, c0 : c0 + width],
+                    lhsT=wa_word_tiles[g][:, 2 * place : 2 * (place + P)].bitcast(FP4X4),
+                    lhsT_scale=wa_scale_tiles[g][:, place : place + P],
+                    rhs=h_codes[half][a][:, c0 : c0 + width].bitcast(FP8X4),
+                    rhs_scale=h_scales[half][a][:, c0 : c0 + width],
                     start=(a == 0),
                     stop=(a == H_PASSES - 1),
                 )
-            if on_vector:
-                nc.vector.tensor_copy(e_sb[i][:, s0 : s0 + width], bank[:, 0:width])
-            else:
-                nc.scalar.copy(e_sb[i][:, s0 : s0 + width], bank[:, 0:width])
+            copy_out(e_sb[i][:, s0 : s0 + width], bank[:, 0:width])
 
-        n_tiles = N_GROUPS * PACK
-        steps = [(0, 0), (1, 0), (0, 1), (0, 2), (1, 1), (1, 2)] + [(ci, b) for ci in (2, 3) for b in range(H_PASSES)]
+        steps = [(ci, b) for ci in range(S // CHUNK) for b in range(H_PASSES)]
+        steps.remove((1, 0))
+        steps = steps[:1] + [(1, 0)] + steps[1:]
         for k, (ci, b) in enumerate(steps):
             stage1(ci, b)
-            if k in (1, 2):
+            if 1 <= k < H_PASSES:
                 quantize_w1(k)
             if k > 0:
                 quantize_h(*steps[k - 1])
         quantize_h(*steps[-1])
         for ci, ahead in enumerate(AHEAD):
             for i in range(ahead):
-                stage2(i, ci * CHUNK, CHUNK, False)
+                stage2(i, ci * CHUNK, CHUNK, nc.scalar.copy)
 
         out0_view = out_0.rearrange("(g p t) m -> g p t m", p=P, t=PACK)
         y_sb = [keep.tile([P, PACK, M], F32, name=f"y{g}") for g in range(N_GROUPS)]
         gate, picked, diff = {}, {}, {}
-        pieces = [(i, 2, 0, M) for i in range(0, n_tiles - 2, 2)]
-        pieces = pieces + [(n_tiles - 2, 1, 0, M), (n_tiles - 1, 1, 0, M // 2), (n_tiles - 1, 1, M // 2, M // 2)]
+        pieces = [(i, 2, 0, M) for i in range(0, ROW_TILES - 2, 2)]
+        pieces = pieces + [(ROW_TILES - 2, 1, 0, M), (ROW_TILES - 1, 1, 0, M // 2), (ROW_TILES - 1, 1, M // 2, M // 2)]
 
         def look(k):
             i0, count, m0, width = pieces[k]
-            cols = slice(m0 // 16, (m0 + width) // 16)
+            cols = slice(m0 // LIST_ROWS, (m0 + width) // LIST_ROWS)
             gate[k] = ring.tile([P, count, width], F32, name="gate")
             picked[k] = ring.tile([P, count, width], F32, name="picked")
             for u in range(count):
@@ -250,57 +268,51 @@ def tile_list_fog_hours_kernel(
                 )
             nc.sync.dma_start(out0_view[g][:, t : t + count, m0 : m0 + width], y_sb[g][:, t : t + count, m0 : m0 + width])
 
-        ybf = {}
-        ys = [keep.tile([P, M], U8, name=f"ys{g}", align_bytes=64) for g in range(N_GROUPS)]
+        y_bf = [keep.tile([P, PACK * M], BF16, name=f"y_bf{g}", align_bytes=64) for g in range(N_GROUPS)]
+        y_scales = [keep.tile([P, M], U8, name=f"y_scales{g}", align_bytes=64) for g in range(N_GROUPS)]
 
-        def round_y(g, m0, width, copy):
-            ybf[(g, m0)] = keep.tile([P, PACK * width], BF16, name=f"ybf{g}_{m0}", align_bytes=64)
-            copy(
-                ybf[(g, m0)][:].rearrange("p (c i t) -> p c t i", i=4, t=PACK),
-                y_sb[g][:, :, m0 : m0 + width].rearrange("p t (c i) -> p c t i", i=4),
+        def round_y(g, m0, width):
+            nc.vector.tensor_copy(
+                y_bf[g][:, PACK * m0 : PACK * (m0 + width)].rearrange("p (c d t) -> p c t d", d=4, t=PACK),
+                y_sb[g][:, :, m0 : m0 + width].rearrange("p t (c d) -> p c t d", d=4),
             )
 
-        def planes(g, m0, width):
-            yc = keep.tile([P, width], I32, name=f"yc{g}_{m0}", align_bytes=64)
-            nc.vector.quantize_mx(out=yc[:].bitcast(FP8X4), scales=ys[g][:, m0 : m0 + width], in_=ybf[(g, m0)][:])
-            nc.sync.dma_start(out_1[g].rearrange("p m t -> p (m t)").bitcast(I32)[:, m0 : m0 + width], yc[:])
-
-        def store_scales(g, queues):
-            for q in range(4):
-                queues[q % len(queues)].dma_start(
-                    out_2[g, 4 * q : 4 * q + 4, :].bitcast(I32), ys[g][32 * q : 32 * q + 4, :].bitcast(I32)
+        def store_planes(g, scale_queues):
+            y_codes = keep.tile([P, M], I32, name=f"y_codes{g}", align_bytes=64)
+            nc.vector.quantize_mx(out=y_codes[:].bitcast(FP8X4), scales=y_scales[g][:], in_=y_bf[g][:])
+            nc.sync.dma_start(out_1[g].rearrange("p m t -> p (m t)").bitcast(I32), y_codes[:])
+            for quad in range(QUADRANTS):
+                scale_queues[quad % len(scale_queues)].dma_start(
+                    out_2[g, 4 * quad : 4 * quad + 4, :].bitcast(I32),
+                    y_scales[g][32 * quad : 32 * quad + 4, :].bitcast(I32),
                 )
 
-        def finish_rows(k):
-            i0, count, m0, width = pieces[k]
+        def finish_rows(i0, count):
             for i in range(i0, i0 + count):
-                if m0 > 0:
-                    continue
                 if i >= AHEAD[1]:
-                    stage2(i, CHUNK, CHUNK, True)
+                    stage2(i, CHUNK, CHUNK, nc.vector.tensor_copy)
                 if i >= AHEAD[2]:
-                    stage2(i, 2 * CHUNK, 2 * CHUNK, False)
+                    stage2(i, 2 * CHUNK, 2 * CHUNK, nc.scalar.copy)
                 else:
-                    stage2(i, 3 * CHUNK, CHUNK, i == 0)
+                    stage2(i, 3 * CHUNK, CHUNK, nc.vector.tensor_copy if i == 0 else nc.scalar.copy)
 
-        finish_rows(0)
+        last_of_group0 = PACK // 2 - 1
+        first_half_piece = len(pieces) - 2
+        finish_rows(*pieces[0][:2])
         for k in range(len(pieces) + 1):
-            if k + 1 < len(pieces):
-                finish_rows(k + 1)
+            if k + 1 <= first_half_piece:
+                finish_rows(*pieces[k + 1][:2])
             if k < len(pieces):
                 look(k)
             if k >= 1:
                 combine(k - 1)
             if k < len(pieces):
                 higher(k)
-            if k - 1 == 1:
-                round_y(0, 0, M, nc.vector.tensor_copy)
-            if k - 1 == 2:
-                planes(0, 0, M)
-                store_scales(0, [nc.sync])
-            if k - 1 == len(pieces) - 2:
-                round_y(1, 0, M // 2, nc.scalar.copy)
-        planes(1, 0, M // 2)
-        round_y(1, M // 2, M // 2, nc.vector.tensor_copy)
-        planes(1, M // 2, M // 2)
-        store_scales(1, [nc.scalar, nc.sync])
+            if k - 1 == last_of_group0:
+                round_y(0, 0, M)
+            if k - 1 == last_of_group0 + 1:
+                store_planes(0, [nc.sync])
+            if k - 1 == first_half_piece:
+                round_y(1, 0, M // 2)
+        round_y(1, M // 2, M // 2)
+        store_planes(1, [nc.scalar, nc.sync])

from contextlib import ExitStack

import concourse.mybir as mybir

K, H, N, T, S, M = 512, 1536, 1024, 4096, 1024, 512
FLOPS = 2 * K * H * S + 2 * H * N * S

F32 = mybir.dt.float32
BF16 = mybir.dt.bfloat16
I32 = mybir.dt.int32
U32 = mybir.dt.uint32
U16 = mybir.dt.uint16
U8 = mybir.dt.uint8
FP8X4 = mybir.dt.float8_e4m3fn_x4
FP4X4 = mybir.dt.float4_e2m1fn_x4
ALU = mybir.AluOpType
ACT = mybir.ActivationFunctionType

P = 128
PACK = 4
PASS = P * PACK
QUADRANTS = 4
LIST_ROWS = 16
H_PASSES = H // PASS
N_GROUPS = N // PASS
ROW_TILES = N_GROUPS * PACK
SUB = 128
CHUNK = 256
AHEAD = (8, 4, 2)
ZERO_SPLIT = 2560

KB = 1024
AT_TABLE_WORDS = 0
AT_WA_WORDS = (0, 3 * KB)
AT_W1 = (16 * KB, 24 * KB, 32 * KB)
AT_TABLE_SCALES = 30 * KB
AT_CLEAR = (8 * KB, 24 * KB)
AT_LIMIT, AT_GAIN = 32 * KB, 32 * KB + 64


def tile_list_fog_hours_kernel(
    tc, tab_words, tab_scales, offs, pos1, pos2, w1, low, wa_words, wa_scales, limit, clear, gain, out_0, out_1, out_2
):
    nc = tc.nc
    with ExitStack() as ctx:
        keep = ctx.enter_context(tc.tile_pool(name="keep", bufs=1))
        share = ctx.enter_context(tc.tile_pool(name="share", bufs=1))
        ring = ctx.enter_context(tc.tile_pool(name="ring", bufs=3))
        ps1 = ctx.enter_context(tc.psum_pool(name="ps1", bufs=4))
        ps2 = ctx.enter_context(tc.psum_pool(name="ps2", bufs=4))

        offs_sb = keep.tile([P, S // LIST_ROWS], U16, name="offs_sb")
        pos1_sb = keep.tile([P, M // LIST_ROWS], U16, name="pos1_sb")
        pos2_sb = keep.tile([P, M // LIST_ROWS], U16, name="pos2_sb")
        table_words = share.tile([P, T], I32, name="table_words", offset=AT_TABLE_WORDS)
        table_scales = share.tile([P, T], U8, name="table_scales", offset=AT_TABLE_SCALES)
        picked_scales = keep.tile([P, S], U8, name="picked_scales")
        wa_scales_raw = keep.tile([P, H_PASSES * PASS], U8, name="wa_scales_raw")
        wa_scales_dealt = keep.tile([P, H_PASSES * PASS], U8, name="wa_scales_dealt")
        wa_scale_tiles = [keep.tile([P, H_PASSES * PASS], U8, name=f"wa_scale_tile{g}", align_bytes=64) for g in range(N_GROUPS)]
        v_scales = keep.tile([P, S], U8, name="v_scales", align_bytes=64)
        low_sb = keep.tile([P, H_PASSES, PACK], F32, name="low_sb")

        nc.gpsimd.memset(table_scales[:, 0:ZERO_SPLIT].bitcast(I32), 0)
        nc.vector.memset(table_scales[:, ZERO_SPLIT:T].bitcast(I32), 0)
        nc.vector.memset(wa_scales_raw[:].bitcast(I32), 0)
        nc.vector.memset(v_scales[:].bitcast(I32), 0)
        for g in range(N_GROUPS):
            nc.vector.memset(wa_scale_tiles[g][:].bitcast(I32), 0)

        w1_view = w1.rearrange("(p j) c -> p j c", j=PACK)
        w1_parts = [[] for b in range(H_PASSES)]

        def load_w1(b, c0, c1):
            raw = share.tile([P, PACK, c1 - c0], F32, name=f"w1_raw{b}_{c0}", offset=AT_W1[b] + 4 * PACK * c0)
            nc.sync.dma_start(raw[:], w1_view[:, :, b * PASS + c0 : b * PASS + c1])
            w1_parts[b].append((c0, c1, raw))

        nc.sync.dma_start(offs_sb[:], offs)
        load_w1(0, 0, PASS // 2)
        load_w1(0, PASS // 2, PASS)
        nc.sync.dma_start(pos1_sb[:], pos1)
        nc.sync.dma_start(table_scales[0:P:8, :].bitcast(I32), tab_scales[0].bitcast(I32))
        nc.sync.dma_start(
            wa_scales_raw[0:P:4, :].bitcast(I32).rearrange("r (a c) -> r a c", a=H_PASSES),
            wa_scales.bitcast(I32).rearrange("a q (g c) -> (q g) a c", g=N_GROUPS),
        )
        nc.sync.dma_start(table_words[:], tab_words[0].rearrange("p n t -> p (n t)").bitcast(I32))
        nc.sync.dma_start(low_sb[:], low.rearrange("(b p t) -> p b t", p=P, t=PACK))
        nc.sync.dma_start(pos2_sb[:], pos2)

        nc.vector.tensor_copy(picked_scales[:], table_scales[:].indirect(offs_sb[:]))
        for quad in range(QUADRANTS):
            nc.sync.dma_start(
                v_scales[32 * quad : 32 * quad + 4, :].bitcast(I32),
                picked_scales[32 * quad : 32 * quad + 32 : 8, :].bitcast(I32),
            )

        w1_codes, w1_scales, w1_bf = [], [], []
        for b in range(H_PASSES):
            w1_bf.append(keep.tile([P, PACK * PASS], BF16, name=f"w1_bf{b}", align_bytes=64))
            w1_codes.append(keep.tile([P, PASS], U32, name=f"w1_codes{b}", align_bytes=64))
            w1_scales.append(keep.tile([P, PASS], U8, name=f"w1_scales{b}", align_bytes=64))

        def round_w1(b):
            dealt = w1_bf[b][:].rearrange("p (t m j) -> p m j t", t=PACK, j=PACK)
            for c0, c1, raw in w1_parts[b]:
                nc.scalar.copy(dealt[:, c0 // PACK : c1 // PACK, :, :], raw[:].rearrange("p j (m t) -> p m j t", t=PACK))

        def quantize_w1(b):
            nc.vector.quantize_mx(out=w1_codes[b][:].bitcast(FP8X4), scales=w1_scales[b][:], in_=w1_bf[b][:])

        for b in range(1, H_PASSES):
            load_w1(b, 0, PASS)

        round_w1(0)
        quantize_w1(0)

        nc.vector.tensor_copy(
            wa_scales_dealt[:].rearrange("p (a t m) -> p a t m", a=H_PASSES, t=PACK),
            wa_scales_raw[:].rearrange("p (a m t) -> p a t m", a=H_PASSES, t=PACK),
        )
        for g, queue in enumerate((nc.sync, nc.gpsimd)):
            for quad in range(QUADRANTS):
                queue.dma_start(
                    wa_scale_tiles[g][32 * quad : 32 * quad + 4, :].bitcast(I32),
                    wa_scales_dealt[32 * quad + 4 * g : 32 * quad + 32 : 8, :].bitcast(I32),
                )

        v_words = []
        for ci in range(S // CHUNK):
            entries = offs_sb[:, ci * CHUNK // LIST_ROWS : (ci + 1) * CHUNK // LIST_ROWS]
            words = keep.tile([P, CHUNK], U32, name=f"v_words{ci}", align_bytes=64)
            nc.vector.tensor_copy(words[:], table_words[:].bitcast(U32).indirect(entries))
            v_words.append(words)

        for b in range(1, H_PASSES):
            round_w1(b)

        wa_words_raw = []
        for g in range(N_GROUPS):
            raw = share.tile([P, H_PASSES * PASS // 2], I32, name=f"wa_words_raw{g}", offset=AT_WA_WORDS[g])
            nc.sync.dma_start(
                raw[:].rearrange("p (a c) -> p a c", a=H_PASSES),
                wa_words[:, :, 2 * g * PASS : 2 * (g + 1) * PASS].bitcast(I32).rearrange("a p c -> p a c"),
            )
            wa_words_raw.append(raw)
        clear_view = clear.rearrange("(g p t) m -> g p t m", p=P, t=PACK)
        clear_sb = []
        for g in range(N_GROUPS):
            rows = share.tile([P, PACK, M], F32, name=f"clear{g}", offset=AT_CLEAR[g])
            nc.sync.dma_start(rows[:], clear_view[g])
            clear_sb.append(rows)
        limit_sb = share.tile([P, ROW_TILES], F32, name="limit_sb", offset=AT_LIMIT)
        gain_sb = share.tile([P, ROW_TILES], F32, name="gain_sb", offset=AT_GAIN)
        nc.sync.dma_start(limit_sb[:].rearrange("p (g t) -> p g t", t=PACK), limit.rearrange("(g p t) -> p g t", p=P, t=PACK))
        nc.sync.dma_start(gain_sb[:].rearrange("p (g t) -> p g t", t=PACK), gain.rearrange("(g p t) -> p g t", p=P, t=PACK))

        wa_word_tiles = []
        for g in range(N_GROUPS):
            dealt_words = keep.tile([P, H_PASSES * 2 * PASS], U8, name=f"wa_word_tile{g}", align_bytes=64)
            nc.scalar.copy(
                dealt_words[:].bitcast(U16).rearrange("p (a t m) -> p a t m", a=H_PASSES, t=PACK),
                wa_words_raw[g][:].bitcast(U16).rearrange("p (a m t) -> p a t m", a=H_PASSES, t=PACK),
            )
            wa_word_tiles.append(dealt_words)

        e_sb = [keep.tile([P, S], F32, name=f"e{i}") for i in range(ROW_TILES)]
        h_codes = [
            [keep.tile([P, S // 2], U32, name=f"h_codes{half}_{b}", align_bytes=64) for b in range(H_PASSES)] for half in range(2)
        ]
        h_scales = [
            [keep.tile([P, S // 2], U8, name=f"h_scales{half}_{b}", align_bytes=64) for b in range(H_PASSES)] for half in range(2)
        ]
        h_bf = {}

        def stage1(ci, b):
            h_bf[(ci, b)] = ring.tile([P, PACK * CHUNK], BF16, name="h_bf", align_bytes=64)
            for u in range(CHUNK // SUB):
                col = ci * CHUNK + u * SUB
                bank = ps1.tile([P, PACK, SUB], F32, name="bank1")
                for t in range(PACK):
                    nc.tensor.matmul_mx(
                        out=bank[:, t, :],
                        lhsT=w1_codes[b][:, t * P : (t + 1) * P].bitcast(FP8X4),
                        lhsT_scale=w1_scales[b][:, t * P : (t + 1) * P],
                        rhs=v_words[ci][:, u * SUB : (u + 1) * SUB].bitcast(FP8X4),
                        rhs_scale=v_scales[:, col : col + SUB],
                        start=True,
                        stop=True,
                    )
                nc.vector.tensor_tensor(
                    h_bf[(ci, b)][:, u * PACK * SUB : (u + 1) * PACK * SUB].rearrange("p (j t) -> p j t", t=PACK),
                    bank[:].rearrange("p t j -> p j t"),
                    low_sb[:, b : b + 1, :].to_broadcast([P, SUB, PACK]),
                    ALU.max,
                )

        def quantize_h(ci, b):
            half, c0 = divmod(ci * CHUNK, S // 2)
            nc.vector.quantize_mx(
                out=h_codes[half][b][:, c0 : c0 + CHUNK].bitcast(FP8X4),
                scales=h_scales[half][b][:, c0 : c0 + CHUNK],
                in_=h_bf[(ci, b)][:],
            )

        def stage2(i, s0, width, copy_out):
            half, c0 = divmod(s0, S // 2)
            g, t = divmod(i, PACK)
            bank = ps2.tile([P, PASS], F32, name="bank2")
            for a in range(H_PASSES):
                place = a * PASS + t * P
                nc.tensor.matmul_mx(
                    out=bank[:, 0:width],
                    lhsT=wa_word_tiles[g][:, 2 * place : 2 * (place + P)].bitcast(FP4X4),
                    lhsT_scale=wa_scale_tiles[g][:, place : place + P],
                    rhs=h_codes[half][a][:, c0 : c0 + width].bitcast(FP8X4),
                    rhs_scale=h_scales[half][a][:, c0 : c0 + width],
                    start=(a == 0),
                    stop=(a == H_PASSES - 1),
                )
            copy_out(e_sb[i][:, s0 : s0 + width], bank[:, 0:width])

        steps = [(ci, b) for ci in range(S // CHUNK) for b in range(H_PASSES)]
        steps.remove((1, 0))
        steps = steps[:1] + [(1, 0)] + steps[1:]
        for k, (ci, b) in enumerate(steps):
            stage1(ci, b)
            if 1 <= k < H_PASSES:
                quantize_w1(k)
            if k > 0:
                quantize_h(*steps[k - 1])
        quantize_h(*steps[-1])
        for ci, ahead in enumerate(AHEAD):
            for i in range(ahead):
                stage2(i, ci * CHUNK, CHUNK, nc.scalar.copy)

        out0_view = out_0.rearrange("(g p t) m -> g p t m", p=P, t=PACK)
        y_sb = [keep.tile([P, PACK, M], F32, name=f"y{g}") for g in range(N_GROUPS)]
        gate, picked, diff = {}, {}, {}
        pieces = [(i, 2, 0, M) for i in range(0, ROW_TILES - 2, 2)]
        pieces = pieces + [(ROW_TILES - 2, 1, 0, M), (ROW_TILES - 1, 1, 0, M // 2), (ROW_TILES - 1, 1, M // 2, M // 2)]

        def look(k):
            i0, count, m0, width = pieces[k]
            cols = slice(m0 // LIST_ROWS, (m0 + width) // LIST_ROWS)
            gate[k] = ring.tile([P, count, width], F32, name="gate")
            picked[k] = ring.tile([P, count, width], F32, name="picked")
            for u in range(count):
                i = i0 + u
                nc.scalar.activation(gate[k][:, u, :], e_sb[i][:].indirect(pos1_sb[:, cols]), ACT.Sigmoid, bias=limit_sb[:, i : i + 1])
                nc.vector.tensor_copy(picked[k][:, u, :], e_sb[i][:].indirect(pos2_sb[:, cols]))

        def higher(k):
            i0, count, m0, width = pieces[k]
            g, t = divmod(i0, PACK)
            nc.vector.tensor_tensor(picked[k][:], picked[k][:], clear_sb[g][:, t : t + count, m0 : m0 + width], ALU.max)

        def combine(k):
            i0, count, m0, width = pieces[k]
            g, t = divmod(i0, PACK)
            diff[k] = ring.tile([P, count, width], F32, name="diff")
            engine = nc.gpsimd if width == M else nc.vector
            engine.tensor_tensor(diff[k][:], picked[k][:], gate[k][:], ALU.subtract)
            for u in range(count):
                nc.scalar.activation(
                    y_sb[g][:, t + u, m0 : m0 + width], diff[k][:, u, :], ACT.Copy, scale=gain_sb[:, i0 + u : i0 + u + 1]
                )
            nc.sync.dma_start(out0_view[g][:, t : t + count, m0 : m0 + width], y_sb[g][:, t : t + count, m0 : m0 + width])

        y_bf = [keep.tile([P, PACK * M], BF16, name=f"y_bf{g}", align_bytes=64) for g in range(N_GROUPS)]
        y_scales = [keep.tile([P, M], U8, name=f"y_scales{g}", align_bytes=64) for g in range(N_GROUPS)]

        def round_y(g, m0, width):
            nc.vector.tensor_copy(
                y_bf[g][:, PACK * m0 : PACK * (m0 + width)].rearrange("p (c d t) -> p c t d", d=4, t=PACK),
                y_sb[g][:, :, m0 : m0 + width].rearrange("p t (c d) -> p c t d", d=4),
            )

        def store_planes(g, scale_queues):
            y_codes = keep.tile([P, M], I32, name=f"y_codes{g}", align_bytes=64)
            nc.vector.quantize_mx(out=y_codes[:].bitcast(FP8X4), scales=y_scales[g][:], in_=y_bf[g][:])
            nc.sync.dma_start(out_1[g].rearrange("p m t -> p (m t)").bitcast(I32), y_codes[:])
            for quad in range(QUADRANTS):
                scale_queues[quad % len(scale_queues)].dma_start(
                    out_2[g, 4 * quad : 4 * quad + 4, :].bitcast(I32),
                    y_scales[g][32 * quad : 32 * quad + 4, :].bitcast(I32),
                )

        def finish_rows(i0, count):
            for i in range(i0, i0 + count):
                if i >= AHEAD[1]:
                    stage2(i, CHUNK, CHUNK, nc.vector.tensor_copy)
                if i >= AHEAD[2]:
                    stage2(i, 2 * CHUNK, 2 * CHUNK, nc.scalar.copy)
                else:
                    stage2(i, 3 * CHUNK, CHUNK, nc.vector.tensor_copy if i == 0 else nc.scalar.copy)

        last_of_group0 = PACK // 2 - 1
        first_half_piece = len(pieces) - 2
        finish_rows(*pieces[0][:2])
        for k in range(len(pieces) + 1):
            if k + 1 <= first_half_piece:
                finish_rows(*pieces[k + 1][:2])
            if k < len(pieces):
                look(k)
            if k >= 1:
                combine(k - 1)
            if k < len(pieces):
                higher(k)
            if k - 1 == last_of_group0:
                round_y(0, 0, M)
            if k - 1 == last_of_group0 + 1:
                store_planes(0, [nc.sync])
            if k - 1 == first_half_piece:
                round_y(1, 0, M // 2)
        round_y(1, M // 2, M // 2)
        store_planes(1, [nc.scalar, nc.sync])
